import numpy as np
import ml_dtypes


def mxq(x, axis, fmt="e4m3"):
    dtype, down = {"e4m3": (ml_dtypes.float8_e4m3fn, 7), "e5m2": (ml_dtypes.float8_e5m2, 14)}[fmt]
    v = np.moveaxis(np.asarray(x, np.float32).astype(ml_dtypes.bfloat16).astype(np.float64), axis, -1)
    blocks = v.reshape(v.shape[:-1] + (-1, 32))
    amax = np.abs(blocks).max(-1, keepdims=True)
    byte = np.maximum(np.where(amax > 0, np.frexp(amax)[1] - 1 + 127, 0) - down, 1)
    scale = np.exp2(byte - 127.0)
    codes = (blocks / scale).astype(np.float32).astype(dtype).astype(np.float64)
    return np.moveaxis((codes * scale).reshape(v.shape), -1, axis)


WIDE = False


def mx_kscale(k):
    if not WIDE:
        return np.ones(k)
    levels = np.array([10, -10, 5, -5, 0])
    if k % 512:
        return np.exp2(np.random.permutation(np.resize(levels, k // 32))).repeat(32)
    a = np.empty((k // 512, 16))
    for p in range(k // 512):
        a[p, :8] = np.random.permutation(np.resize(levels, 8))
        for g in range(8):
            far = levels[np.abs(levels - a[p, g]) >= 10]
            a[p, g + 8] = far[np.random.randint(len(far))]
    return np.exp2(a.ravel()).repeat(32)


def f64(x):
    return np.asarray(x).astype(np.float64)


def striped(idx):
    return np.tile(idx.reshape(-1, 16).T, (8, 1)).astype(np.uint16)


def unstriped(offs):
    return offs[:16].T.reshape(-1).astype(np.int64)


def pack_weight(w):
    k, n = w.shape
    w = f64(np.asarray(w, np.float32).astype(ml_dtypes.bfloat16)).reshape(k // 32, 32, n)
    amax = np.abs(w).max(1)
    byte = np.clip(np.where(amax > 0, np.frexp(amax)[1] - 1 + 127 - 7, 1), 1, 254)
    scaled = (w * np.exp2(127.0 - byte)[:, None, :]).reshape(k, n).astype(np.float32)
    words = np.ascontiguousarray(scaled.reshape(k // 512, 128, 4, n).transpose(0, 1, 3, 2)).astype(ml_dtypes.float8_e4m3fn).view(np.uint8)
    return words, np.ascontiguousarray(byte.astype(np.uint8).reshape(k // 512, 16, n))


def unpack_weight(words, scales):
    g, p, n, _ = words.shape
    vals = np.ascontiguousarray(words).view(ml_dtypes.float8_e4m3fn).astype(np.float64) * np.repeat(np.exp2(scales.astype(np.float64) - 127.0), 8, axis=1)[..., None]
    return vals.transpose(0, 1, 3, 2).reshape(g * 512, n)


def relu(v):
    return np.maximum(v, 0.0)


K, T, S, D, N, V = 1024, 2048, 512, 4, 128, 128


def setup_inputs():
    n = np.random.standard_normal
    s = mx_kscale(K)[:, None]
    packed_xT = pack_weight(n((K, T)) * s)
    return {
        "x_words": packed_xT[0],
        "x_scales": packed_xT[1],
        "w1": (n((K, N)) / np.sqrt(K) / s).astype(np.float32),
        "w2": (n((K, N)) / np.sqrt(K) / s).astype(np.float32),
        "unom": (n((N, V))).astype(np.float32),
        "offs": striped(np.random.permutation(T)[:S]),
    }


def reference(x_words, x_scales, w1, w2, unom, offs):
    xq = unpack_weight(x_words, x_scales)[:, unstriped(offs)]
    yg = mxq(f64(w2), 0, "e4m3").T @ xq
    yh = mxq(f64(w1), 0, "e4m3").T @ xq
    bar = np.exp(0.4 * yh)
    slack = yg * (np.repeat(f64(unom), D, axis=1)) + 0.8 * (bar - 1.0)
    mult = relu(-1.0 * slack) / ((yg) ** 2 + 0.3)
    kg = mult * yg
    return f64(unom) + kg.reshape(len(kg), -1, D).sum(axis=2)

@@ -1,0 +1,147 @@
+from contextlib import ExitStack
+
+import concourse.mybir as mybir
+
+K, T, S, D, N, V = 1024, 2048, 512, 4, 128, 128
+FLOPS = 2 * 2 * K * N * S
+
+F32 = mybir.dt.float32
+BF16 = mybir.dt.bfloat16
+I32 = mybir.dt.int32
+U32 = mybir.dt.uint32
+U16 = mybir.dt.uint16
+U8 = mybir.dt.uint8
+FP8X4 = mybir.dt.float8_e4m3fn_x4
+ALU = mybir.AluOpType
+ACT = mybir.ActivationFunctionType
+
+P = 128
+PACK = 4
+PASSES = K // (P * PACK)
+HALF = S // 2
+SLOTS = 8
+
+
+def tile_picked_ycbf_sum_p_kernel(tc, x_words, x_scales, w1, w2, unom, offs, out):
+    nc = tc.nc
+    with ExitStack() as ctx:
+        sb = ctx.enter_context(tc.tile_pool(name="sb", bufs=1))
+        ps = ctx.enter_context(tc.psum_pool(name="ps", bufs=1))
+
+        offsets = sb.tile([P, S // 16], U16, name="offsets")
+        table_scales = sb.tile([P, T], U8, name="table_scales", align_bytes=64)
+        table_words = [sb.tile([P, T], U32, name=f"table_words{g}", align_bytes=64) for g in range(PASSES)]
+        w2_raw = sb.tile([P, PASSES, PACK * N], F32, name="w2_raw")
+        w1_raw = [sb.tile([P, PACK * N], F32, name=f"w1_raw{g}") for g in range(PASSES)]
+        u = sb.tile([P, V], F32, name="u")
+        warm = sb.tile([P, 8], F32, name="warm")
+        warm_out = sb.tile([P, 8], F32, name="warm_out")
+
+        nc.vector.memset(table_scales[:].bitcast(I32), 0)
+        nc.vector.memset(warm[:], 1.0)
+
+        nc.sync.dma_start(w2_raw[:], w2.rearrange("(g p j) m -> p g (j m)", g=PASSES, j=PACK))
+        for q in range(4):
+            nc.sync.dma_start(
+                table_scales[32 * q : 32 * q + 4 * PASSES, :].bitcast(I32),
+                x_scales[:, 4 * q : 4 * q + 4, :].bitcast(I32),
+            )
+        nc.sync.dma_start(offsets[:], offs)
+        nc.scalar.activation(warm_out[:, 0:1], warm[:, 0:1], ACT.Abs_reciprocal_sqrt)
+        for g in range(PASSES):
+            nc.sync.dma_start(table_words[g][:].bitcast(I32), x_words[g].rearrange("p n t -> p (n t)").bitcast(I32))
+        nc.sync.dma_start(u[:], unom)
+        w1_view = w1.rearrange("(g p j) m -> g p (j m)", g=PASSES, j=PACK)
+        for g in range(PASSES):
+            nc.sync.dma_start(w1_raw[g][:], w1_view[g])
+
+        w2_bf = sb.tile([P, PASSES, N, PACK], BF16, name="w2_bf", align_bytes=64)
+        for g in range(PASSES):
+            nc.vector.tensor_copy(w2_bf[:, g, :, :], w2_raw[:, g, :].rearrange("p (j m) -> p m j", j=PACK))
+        w2_codes = sb.tile([P, PASSES * N], U32, name="w2_codes", align_bytes=64)
+        w2_scales = sb.tile([P, PASSES * N], U8, name="w2_scales", align_bytes=64)
+        nc.vector.quantize_mx(
+            out=w2_codes[:].bitcast(FP8X4), scales=w2_scales[:], in_=w2_bf[:].rearrange("p g m j -> p (g m j)")
+        )
+
+        picked_scales = sb.tile([P, S], U8, name="picked_scales", align_bytes=64)
+        nc.vector.tensor_copy(picked_scales[:], table_scales[:].indirect(offsets[:]))
+        picked0 = sb.tile([P, S], U32, name="picked0", align_bytes=64)
+        nc.vector.tensor_copy(picked0[:], table_words[0][:].indirect(offsets[:]))
+
+        terms = sb.tile([P, V, SLOTS], F32, name="terms")
+        nc.scalar.copy(terms[:, :, D], u[:])
+
+        picked1 = sb.tile([P, S], U32, name="picked1", align_bytes=64)
+        picked = [picked0, picked1]
+        yg = [ps.tile([P, HALF], F32, name=f"yg{h}") for h in range(2)]
+        yh = ps.tile([P, S], F32, name="yh")
+        sq = [sb.tile([P, HALF], F32, name=f"sq{h}") for h in range(2)]
+        rs = [sb.tile([P, HALF], F32, name=f"rs{h}") for h in range(2)]
+
+        def mm(acc, codes, scales, g, cols):
+            nc.tensor.matmul_mx(
+                out=acc,
+                lhsT=codes.bitcast(FP8X4),
+                lhsT_scale=scales,
+                rhs=picked[g][:, cols].bitcast(FP8X4),
+                rhs_scale=picked_scales[4 * g : P, cols],
+                start=(g == 0),
+                stop=(g == PASSES - 1),
+            )
+
+        for h in range(2):
+            mm(yg[h][:], w2_codes[:, 0:N], w2_scales[:, 0:N], 0, slice(h * HALF, (h + 1) * HALF))
+        for h in range(2):
+            cols = slice(h * HALF, (h + 1) * HALF)
+            nc.vector.tensor_copy(
+                picked1[:, cols], table_words[1][:].indirect(offsets[:, h * HALF // 16 : (h + 1) * HALF // 16])
+            )
+            mm(yg[h][:], w2_codes[:, N : 2 * N], w2_scales[:, N : 2 * N], 1, cols)
+            nc.scalar.activation(sq[h][:], yg[h][:], ACT.Square)
+            nc.scalar.activation(rs[h][:], sq[h][:], ACT.Abs_reciprocal_sqrt, bias=0.3)
+
+        w1_bf = [sb.tile([P, N, PACK], BF16, name=f"w1_bf{g}", align_bytes=64) for g in range(PASSES)]
+        w1_codes = [sb.tile([P, N], U32, name=f"w1_codes{g}", align_bytes=64) for g in range(PASSES)]
+        w1_scales = [sb.tile([P, N], U8, name=f"w1_scales{g}", align_bytes=64) for g in range(PASSES)]
+        for g in range(PASSES):
+            nc.vector.tensor_copy(w1_bf[g][:], w1_raw[g][:].rearrange("p (j m) -> p m j", j=PACK))
+        for g in range(PASSES):
+            nc.vector.quantize_mx(
+                out=w1_codes[g][:].bitcast(FP8X4), scales=w1_scales[g][:], in_=w1_bf[g][:].rearrange("p m j -> p (m j)")
+            )
+            mm(yh[:], w1_codes[g][:], w1_scales[g][:], g, slice(0, S))
+
+        VH = V // 2
+        push = [sb.tile([P, HALF], F32, name=f"push{h}") for h in range(2)]
+        part = [sb.tile([P, HALF], F32, name=f"part{h}") for h in range(2)]
+        gain = [sb.tile([P, HALF], F32, name=f"gain{h}") for h in range(2)]
+        bar = [sb.tile([P, HALF], F32, name=f"bar{h}") for h in range(2)]
+        slack = [sb.tile([P, HALF], F32, name=f"slack{h}") for h in range(2)]
+        res = [sb.tile([P, VH], F32, name=f"res{h}") for h in range(2)]
+
+        def by_state(ap):
+            return ap.rearrange("p (v d) -> p v d", d=D)
+
+        for h in range(2):
+            states = slice(h * VH, (h + 1) * VH)
+            nc.vector.scalar_tensor_tensor(
+                by_state(push[h][:]), by_state(yg[h][:]), 1.25,
+                u[:, states].unsqueeze(2).to_broadcast([P, VH, D]), ALU.mult, ALU.mult,
+            )
+            nc.vector.tensor_tensor(part[h][:], yg[h][:], rs[h][:], ALU.mult)
+        for h in range(2):
+            nc.vector.scalar_tensor_tensor(gain[h][:], part[h][:], -0.8, rs[h][:], ALU.mult, ALU.mult)
+        for h in range(2):
+            nc.scalar.activation(bar[h][:], yh[:, h * HALF : (h + 1) * HALF], ACT.Exp, scale=0.4)
+        for h in range(2):
+            nc.vector.scalar_tensor_tensor(slack[h][:], push[h][:], 1.0, bar[h][:], ALU.subtract, ALU.add)
+        for h in range(2):
+            states = slice(h * VH, (h + 1) * VH)
+            nc.vector.scalar_tensor_tensor(
+                terms[:, states, 0:D], by_state(slack[h][:]), 0.0, by_state(gain[h][:]), ALU.min, ALU.mult
+            )
+        for h in range(2):
+            states = slice(h * VH, (h + 1) * VH)
+            nc.vector.tensor_reduce(res[h][:], terms[:, states, 0 : D + 1], mybir.AxisListType.X, ALU.add)
+            nc.sync.dma_start(out[:, states], res[h][:])

@@ -29,10 +29,10 @@ def tile_picked_ycbf_sum_p_kernel(tc, x_words, x_scales, w1, w2, unom, offs, out
         ps = ctx.enter_context(tc.psum_pool(name="ps", bufs=1))
 
         offsets = sb.tile([P, S // 16], U16, name="offsets")
-        table_scales = sb.tile([P, T], U8, name="table_scales", align_bytes=64)
+        table_scales = sb.tile([P, T], U8, name="table_scales", tag="bytes", align_bytes=64)
         table_words = [sb.tile([P, T], U32, name=f"table_words{g}", align_bytes=64) for g in range(PASSES)]
         w2_raw = sb.tile([P, PASSES, PACK * N], F32, name="w2_raw")
-        w1_raw = [sb.tile([P, PACK * N], F32, name=f"w1_raw{g}") for g in range(PASSES)]
+        w1_raw = [sb.tile([P, PACK * N], F32, name=f"w1_raw{g}", tag=f"raw{g}") for g in range(PASSES)]
         u = sb.tile([P, V], F32, name="u")
         warm = sb.tile([P, 8], F32, name="warm")
         warm_out = sb.tile([P, 8], F32, name="warm_out")
@@ -40,16 +40,19 @@ def tile_picked_ycbf_sum_p_kernel(tc, x_words, x_scales, w1, w2, unom, offs, out
         nc.vector.memset(table_scales[:].bitcast(I32), 0)
         nc.vector.memset(warm[:], 1.0)
 
-        nc.sync.dma_start(w2_raw[:], w2.rearrange("(g p j) m -> p g (j m)", g=PASSES, j=PACK))
+        def load_words(g):
+            nc.sync.dma_start(table_words[g][:].bitcast(I32), x_words[g].rearrange("p n t -> p (n t)").bitcast(I32))
+
+        load_words(0)
+        nc.sync.dma_start(offsets[:], offs)
         for q in range(4):
             nc.sync.dma_start(
                 table_scales[32 * q : 32 * q + 4 * PASSES, :].bitcast(I32),
                 x_scales[:, 4 * q : 4 * q + 4, :].bitcast(I32),
             )
-        nc.sync.dma_start(offsets[:], offs)
         nc.scalar.activation(warm_out[:, 0:1], warm[:, 0:1], ACT.Abs_reciprocal_sqrt)
-        for g in range(PASSES):
-            nc.sync.dma_start(table_words[g][:].bitcast(I32), x_words[g].rearrange("p n t -> p (n t)").bitcast(I32))
+        nc.sync.dma_start(w2_raw[:], w2.rearrange("(g p j) m -> p g (j m)", g=PASSES, j=PACK))
+        load_words(1)
         nc.sync.dma_start(u[:], unom)
         w1_view = w1.rearrange("(g p j) m -> g p (j m)", g=PASSES, j=PACK)
         for g in range(PASSES):
@@ -57,7 +60,7 @@ def tile_picked_ycbf_sum_p_kernel(tc, x_words, x_scales, w1, w2, unom, offs, out
 
         w2_bf = sb.tile([P, PASSES, N, PACK], BF16, name="w2_bf", align_bytes=64)
         for g in range(PASSES):
-            nc.vector.tensor_copy(w2_bf[:, g, :, :], w2_raw[:, g, :].rearrange("p (j m) -> p m j", j=PACK))
+            nc.scalar.copy(w2_bf[:, g, :, :], w2_raw[:, g, :].rearrange("p (j m) -> p m j", j=PACK))
         w2_codes = sb.tile([P, PASSES * N], U32, name="w2_codes", align_bytes=64)
         w2_scales = sb.tile([P, PASSES * N], U8, name="w2_scales", align_bytes=64)
         nc.vector.quantize_mx(
@@ -72,7 +75,7 @@ def tile_picked_ycbf_sum_p_kernel(tc, x_words, x_scales, w1, w2, unom, offs, out
         terms = sb.tile([P, V, SLOTS], F32, name="terms")
         nc.scalar.copy(terms[:, :, D], u[:])
 
-        picked1 = sb.tile([P, S], U32, name="picked1", align_bytes=64)
+        picked1 = sb.tile([P, S], U32, name="picked1", tag="bytes", align_bytes=64)
         picked = [picked0, picked1]
         yg = [ps.tile([P, HALF], F32, name=f"yg{h}") for h in range(2)]
         yh = ps.tile([P, S], F32, name="yh")
@@ -101,7 +104,7 @@ def tile_picked_ycbf_sum_p_kernel(tc, x_words, x_scales, w1, w2, unom, offs, out
             nc.scalar.activation(sq[h][:], yg[h][:], ACT.Square)
             nc.scalar.activation(rs[h][:], sq[h][:], ACT.Abs_reciprocal_sqrt, bias=0.3)
 
-        w1_bf = [sb.tile([P, N, PACK], BF16, name=f"w1_bf{g}", align_bytes=64) for g in range(PASSES)]
+        w1_bf = [sb.tile([P, N, PACK], BF16, name=f"w1_bf{g}", tag=f"bf{g}", align_bytes=64) for g in range(PASSES)]
         w1_codes = [sb.tile([P, N], U32, name=f"w1_codes{g}", align_bytes=64) for g in range(PASSES)]
         w1_scales = [sb.tile([P, N], U8, name=f"w1_scales{g}", align_bytes=64) for g in range(PASSES)]
         for g in range(PASSES):
@@ -113,8 +116,10 @@ def tile_picked_ycbf_sum_p_kernel(tc, x_words, x_scales, w1, w2, unom, offs, out
             mm(yh[:], w1_codes[g][:], w1_scales[g][:], g, slice(0, S))
 
         VH = V // 2
-        push = [sb.tile([P, HALF], F32, name=f"push{h}") for h in range(2)]
-        part = [sb.tile([P, HALF], F32, name=f"part{h}") for h in range(2)]
+        push0 = sb.tile([P, HALF], F32, name="push0", tag="raw1")
+        late = sb.tile([P, 3, HALF], F32, name="late", tag="bf1", align_bytes=64)
+        push = [push0[:], late[:, 0, :]]
+        part = [late[:, 1, :], late[:, 2, :]]
         gain = [sb.tile([P, HALF], F32, name=f"gain{h}") for h in range(2)]
         bar = [sb.tile([P, HALF], F32, name=f"bar{h}") for h in range(2)]
         slack = [sb.tile([P, HALF], F32, name=f"slack{h}") for h in range(2)]
@@ -126,16 +131,16 @@ def tile_picked_ycbf_sum_p_kernel(tc, x_words, x_scales, w1, w2, unom, offs, out
         for h in range(2):
             states = slice(h * VH, (h + 1) * VH)
             nc.vector.scalar_tensor_tensor(
-                by_state(push[h][:]), by_state(yg[h][:]), 1.25,
+                by_state(push[h]), by_state(yg[h][:]), 1.25,
                 u[:, states].unsqueeze(2).to_broadcast([P, VH, D]), ALU.mult, ALU.mult,
             )
-            nc.vector.tensor_tensor(part[h][:], yg[h][:], rs[h][:], ALU.mult)
+            nc.vector.tensor_tensor(part[h], yg[h][:], rs[h][:], ALU.mult)
         for h in range(2):
-            nc.vector.scalar_tensor_tensor(gain[h][:], part[h][:], -0.8, rs[h][:], ALU.mult, ALU.mult)
+            nc.vector.scalar_tensor_tensor(gain[h][:], part[h], -0.8, rs[h][:], ALU.mult, ALU.mult)
         for h in range(2):
             nc.scalar.activation(bar[h][:], yh[:, h * HALF : (h + 1) * HALF], ACT.Exp, scale=0.4)
         for h in range(2):
-            nc.vector.scalar_tensor_tensor(slack[h][:], push[h][:], 1.0, bar[h][:], ALU.subtract, ALU.add)
+            nc.vector.scalar_tensor_tensor(slack[h][:], push[h], 1.0, bar[h][:], ALU.subtract, ALU.add)
         for h in range(2):
             states = slice(h * VH, (h + 1) * VH)
             nc.vector.scalar_tensor_tensor(

@@ -43,16 +43,20 @@ def tile_picked_ycbf_sum_p_kernel(tc, x_words, x_scales, w1, w2, unom, offs, out
         def load_words(g):
             nc.sync.dma_start(table_words[g][:].bitcast(I32), x_words[g].rearrange("p n t -> p (n t)").bitcast(I32))
 
-        load_words(0)
+        def load_scales(r):
+            for g in range(PASSES):
+                nc.sync.dma_start(
+                    table_scales[4 * g + r : P : 32, :].bitcast(I32), x_scales[g, r : 16 : 4, :].bitcast(I32)
+                )
+
         nc.sync.dma_start(offsets[:], offs)
-        for q in range(4):
-            nc.sync.dma_start(
-                table_scales[32 * q : 32 * q + 4 * PASSES, :].bitcast(I32),
-                x_scales[:, 4 * q : 4 * q + 4, :].bitcast(I32),
-            )
-        nc.scalar.activation(warm_out[:, 0:1], warm[:, 0:1], ACT.Abs_reciprocal_sqrt)
         nc.sync.dma_start(w2_raw[:], w2.rearrange("(g p j) m -> p g (j m)", g=PASSES, j=PACK))
+        load_scales(0)
+        load_words(0)
+        for r in range(1, 4):
+            load_scales(r)
         load_words(1)
+        nc.scalar.activation(warm_out[:, 0:1], warm[:, 0:1], ACT.Abs_reciprocal_sqrt)
         nc.sync.dma_start(u[:], unom)
         w1_view = w1.rearrange("(g p j) m -> g p (j m)", g=PASSES, j=PACK)
         for g in range(PASSES):

@@ -18,8 +18,14 @@ ACT = mybir.ActivationFunctionType
 P = 128
 PACK = 4
 PASSES = K // (P * PACK)
+QUADRANT = 32
+SCALE_ROWS = 4
+LIST_ROWS = 16
 HALF = S // 2
-SLOTS = 8
+PIECE = HALF // 2
+STATES = V // 2
+TERM_PITCH = 8
+YG_GROUPS = ((0, 0, PIECE), (0, PIECE, HALF), (1, 0, HALF))
 
 
 def tile_picked_ycbf_sum_p_kernel(tc, x_words, x_scales, w1, w2, unom, offs, out):
@@ -28,17 +34,17 @@ def tile_picked_ycbf_sum_p_kernel(tc, x_words, x_scales, w1, w2, unom, offs, out
         sb = ctx.enter_context(tc.tile_pool(name="sb", bufs=1))
         ps = ctx.enter_context(tc.psum_pool(name="ps", bufs=1))
 
-        offsets = sb.tile([P, S // 16], U16, name="offsets")
-        table_scales = sb.tile([P, T], U8, name="table_scales", tag="bytes", align_bytes=64)
+        offsets = sb.tile([P, S // LIST_ROWS], U16, name="offsets")
+        table_scales = sb.tile([P, T], U8, name="table_scales", tag="scale_table", align_bytes=64)
         table_words = [sb.tile([P, T], U32, name=f"table_words{g}", align_bytes=64) for g in range(PASSES)]
         w2_raw = sb.tile([P, PASSES, PACK * N], F32, name="w2_raw")
-        w1_raw = [sb.tile([P, PACK * N], F32, name=f"w1_raw{g}", tag=f"raw{g}") for g in range(PASSES)]
+        w1_raw = [sb.tile([P, PACK * N], F32, name=f"w1_raw{g}", tag=f"w1_raw{g}") for g in range(PASSES)]
         u = sb.tile([P, V], F32, name="u")
-        warm = sb.tile([P, 8], F32, name="warm")
-        warm_out = sb.tile([P, 8], F32, name="warm_out")
+        one = sb.tile([P, 1], F32, name="one")
+        inv_weight = sb.tile([P, 1], F32, name="inv_weight")
 
         nc.vector.memset(table_scales[:].bitcast(I32), 0)
-        nc.vector.memset(warm[:], 1.0)
+        nc.vector.memset(one[:], 1.0)
 
         def load_words(g):
             nc.sync.dma_start(table_words[g][:].bitcast(I32), x_words[g].rearrange("p n t -> p (n t)").bitcast(I32))
@@ -46,21 +52,22 @@ def tile_picked_ycbf_sum_p_kernel(tc, x_words, x_scales, w1, w2, unom, offs, out
         def load_scales(r):
             for g in range(PASSES):
                 nc.sync.dma_start(
-                    table_scales[4 * g + r : P : 32, :].bitcast(I32), x_scales[g, r : 16 : 4, :].bitcast(I32)
+                    table_scales[SCALE_ROWS * g + r : P : QUADRANT, :].bitcast(I32),
+                    x_scales[g, r : P // 8 : SCALE_ROWS, :].bitcast(I32),
                 )
 
-        nc.sync.dma_start(offsets[:], offs)
         nc.sync.dma_start(w2_raw[:], w2.rearrange("(g p j) m -> p g (j m)", g=PASSES, j=PACK))
+        nc.sync.dma_start(offsets[:], offs)
         load_scales(0)
         load_words(0)
-        for r in range(1, 4):
+        for r in range(1, SCALE_ROWS):
             load_scales(r)
         load_words(1)
-        nc.scalar.activation(warm_out[:, 0:1], warm[:, 0:1], ACT.Abs_reciprocal_sqrt)
+        nc.scalar.activation(inv_weight[:], one[:], ACT.Abs_reciprocal_sqrt, scale=0.8 * 0.8)
         nc.sync.dma_start(u[:], unom)
-        w1_view = w1.rearrange("(g p j) m -> g p (j m)", g=PASSES, j=PACK)
+        w1_passes = w1.rearrange("(g p j) m -> g p (j m)", g=PASSES, j=PACK)
         for g in range(PASSES):
-            nc.sync.dma_start(w1_raw[g][:], w1_view[g])
+            nc.sync.dma_start(w1_raw[g][:], w1_passes[g])
 
         w2_bf = sb.tile([P, PASSES, N, PACK], BF16, name="w2_bf", align_bytes=64)
         for g in range(PASSES):
@@ -75,40 +82,44 @@ def tile_picked_ycbf_sum_p_kernel(tc, x_words, x_scales, w1, w2, unom, offs, out
         nc.vector.tensor_copy(picked_scales[:], table_scales[:].indirect(offsets[:]))
         picked0 = sb.tile([P, S], U32, name="picked0", align_bytes=64)
         nc.vector.tensor_copy(picked0[:], table_words[0][:].indirect(offsets[:]))
-
-        terms = sb.tile([P, V, SLOTS], F32, name="terms")
-        nc.scalar.copy(terms[:, :, D], u[:])
-
-        picked1 = sb.tile([P, S], U32, name="picked1", tag="bytes", align_bytes=64)
+        picked1 = sb.tile([P, S], U32, name="picked1", tag="scale_table", align_bytes=64)
         picked = [picked0, picked1]
-        yg = [ps.tile([P, HALF], F32, name=f"yg{h}") for h in range(2)]
-        yh = ps.tile([P, S], F32, name="yh")
-        sq = [sb.tile([P, HALF], F32, name=f"sq{h}") for h in range(2)]
-        rs = [sb.tile([P, HALF], F32, name=f"rs{h}") for h in range(2)]
 
-        def mm(acc, codes, scales, g, cols):
+        yg = [ps.tile([P, b - a], F32, name=f"yg{i}") for i, (h, a, b) in enumerate(YG_GROUPS)]
+        yh = ps.tile([P, S], F32, name="yh")
+        square = sb.tile([P, HALF], F32, name="square")
+        root = [sb.tile([P, HALF], F32, name=f"root{h}") for h in range(2)]
+
+        def mx_pass(acc, codes, scales, g, cols):
             nc.tensor.matmul_mx(
                 out=acc,
                 lhsT=codes.bitcast(FP8X4),
                 lhsT_scale=scales,
                 rhs=picked[g][:, cols].bitcast(FP8X4),
-                rhs_scale=picked_scales[4 * g : P, cols],
+                rhs_scale=picked_scales[SCALE_ROWS * g : P, cols],
                 start=(g == 0),
                 stop=(g == PASSES - 1),
             )
 
+        for i, (h, a, b) in enumerate(YG_GROUPS):
+            mx_pass(yg[i][:], w2_codes[:, 0:N], w2_scales[:, 0:N], 0, slice(h * HALF + a, h * HALF + b))
         for h in range(2):
-            mm(yg[h][:], w2_codes[:, 0:N], w2_scales[:, 0:N], 0, slice(h * HALF, (h + 1) * HALF))
-        for h in range(2):
-            cols = slice(h * HALF, (h + 1) * HALF)
             nc.vector.tensor_copy(
-                picked1[:, cols], table_words[1][:].indirect(offsets[:, h * HALF // 16 : (h + 1) * HALF // 16])
+                picked1[:, h * HALF : (h + 1) * HALF],
+                table_words[1][:].indirect(offsets[:, h * HALF // LIST_ROWS : (h + 1) * HALF // LIST_ROWS]),
             )
-            mm(yg[h][:], w2_codes[:, N : 2 * N], w2_scales[:, N : 2 * N], 1, cols)
-            nc.scalar.activation(sq[h][:], yg[h][:], ACT.Square)
-            nc.scalar.activation(rs[h][:], sq[h][:], ACT.Abs_reciprocal_sqrt, bias=0.3)
+            for i, (group_half, a, b) in enumerate(YG_GROUPS):
+                if group_half == h:
+                    cols = slice(h * HALF + a, h * HALF + b)
+                    mx_pass(yg[i][:], w2_codes[:, N : 2 * N], w2_scales[:, N : 2 * N], 1, cols)
+                    for c in range(a, b, PIECE):
+                        nc.scalar.activation(square[:, c : c + PIECE], yg[i][:, c - a : c - a + PIECE], ACT.Square)
+            for c in range(0, HALF, PIECE):
+                nc.scalar.activation(
+                    root[h][:, c : c + PIECE], square[:, c : c + PIECE], ACT.Abs_reciprocal_sqrt, bias=0.3
+                )
 
-        w1_bf = [sb.tile([P, N, PACK], BF16, name=f"w1_bf{g}", tag=f"bf{g}", align_bytes=64) for g in range(PASSES)]
+        w1_bf = [sb.tile([P, N, PACK], BF16, name=f"w1_bf{g}", tag=f"w1_bf{g}", align_bytes=64) for g in range(PASSES)]
         w1_codes = [sb.tile([P, N], U32, name=f"w1_codes{g}", align_bytes=64) for g in range(PASSES)]
         w1_scales = [sb.tile([P, N], U8, name=f"w1_scales{g}", align_bytes=64) for g in range(PASSES)]
         for g in range(PASSES):
@@ -117,40 +128,45 @@ def tile_picked_ycbf_sum_p_kernel(tc, x_words, x_scales, w1, w2, unom, offs, out
             nc.vector.quantize_mx(
                 out=w1_codes[g][:].bitcast(FP8X4), scales=w1_scales[g][:], in_=w1_bf[g][:].rearrange("p m j -> p (m j)")
             )
-            mm(yh[:], w1_codes[g][:], w1_scales[g][:], g, slice(0, S))
+            mx_pass(yh[:], w1_codes[g][:], w1_scales[g][:], g, slice(0, S))
 
-        VH = V // 2
-        push0 = sb.tile([P, HALF], F32, name="push0", tag="raw1")
-        late = sb.tile([P, 3, HALF], F32, name="late", tag="bf1", align_bytes=64)
-        push = [push0[:], late[:, 0, :]]
-        part = [late[:, 1, :], late[:, 2, :]]
+        terms = sb.tile([P, V, TERM_PITCH], F32, name="terms", tag="w1_raw0")
+        nc.vector.tensor_copy(terms[:, :, D], u[:])
+        push0 = sb.tile([P, HALF], F32, name="push0", tag="w1_raw1")
+        after_w1 = sb.tile([P, 3, HALF], F32, name="after_w1", tag="w1_bf1", align_bytes=64)
+        push = [push0[:], after_w1[:, 0, :]]
+        slope = [after_w1[:, 1, :], after_w1[:, 2, :]]
         gain = [sb.tile([P, HALF], F32, name=f"gain{h}") for h in range(2)]
         bar = [sb.tile([P, HALF], F32, name=f"bar{h}") for h in range(2)]
         slack = [sb.tile([P, HALF], F32, name=f"slack{h}") for h in range(2)]
-        res = [sb.tile([P, VH], F32, name=f"res{h}") for h in range(2)]
+        result = [sb.tile([P, STATES], F32, name=f"result{h}") for h in range(2)]
 
         def by_state(ap):
             return ap.rearrange("p (v d) -> p v d", d=D)
 
-        for h in range(2):
-            states = slice(h * VH, (h + 1) * VH)
+        for i, (h, a, b) in enumerate(YG_GROUPS):
+            states = slice((h * HALF + a) // D, (h * HALF + b) // D)
             nc.vector.scalar_tensor_tensor(
-                by_state(push[h]), by_state(yg[h][:]), 1.25,
-                u[:, states].unsqueeze(2).to_broadcast([P, VH, D]), ALU.mult, ALU.mult,
+                by_state(push[h][:, a:b]),
+                by_state(yg[i][:]),
+                inv_weight[:],
+                u[:, states].unsqueeze(2).to_broadcast([P, (b - a) // D, D]),
+                ALU.mult,
+                ALU.mult,
             )
-            nc.vector.tensor_tensor(part[h], yg[h][:], rs[h][:], ALU.mult)
+            nc.vector.tensor_tensor(slope[h][:, a:b], yg[i][:], root[h][:, a:b], ALU.mult)
         for h in range(2):
-            nc.vector.scalar_tensor_tensor(gain[h][:], part[h], -0.8, rs[h][:], ALU.mult, ALU.mult)
+            nc.vector.scalar_tensor_tensor(gain[h][:], slope[h], -0.8, root[h][:], ALU.mult, ALU.mult)
         for h in range(2):
             nc.scalar.activation(bar[h][:], yh[:, h * HALF : (h + 1) * HALF], ACT.Exp, scale=0.4)
         for h in range(2):
             nc.vector.scalar_tensor_tensor(slack[h][:], push[h], 1.0, bar[h][:], ALU.subtract, ALU.add)
         for h in range(2):
-            states = slice(h * VH, (h + 1) * VH)
+            states = slice(h * STATES, (h + 1) * STATES)
             nc.vector.scalar_tensor_tensor(
                 terms[:, states, 0:D], by_state(slack[h][:]), 0.0, by_state(gain[h][:]), ALU.min, ALU.mult
             )
         for h in range(2):
-            states = slice(h * VH, (h + 1) * VH)
-            nc.vector.tensor_reduce(res[h][:], terms[:, states, 0 : D + 1], mybir.AxisListType.X, ALU.add)
-            nc.sync.dma_start(out[:, states], res[h][:])
+            states = slice(h * STATES, (h + 1) * STATES)
+            nc.vector.tensor_reduce(result[h][:], terms[:, states, 0 : D + 1], mybir.AxisListType.X, ALU.add)
+            nc.sync.dma_start(out[:, states], result[h][:])

from contextlib import ExitStack

import concourse.mybir as mybir

K, T, S, D, N, V = 1024, 2048, 512, 4, 128, 128
FLOPS = 2 * 2 * K * N * S

F32 = mybir.dt.float32
BF16 = mybir.dt.bfloat16
I32 = mybir.dt.int32
U32 = mybir.dt.uint32
U16 = mybir.dt.uint16
U8 = mybir.dt.uint8
FP8X4 = mybir.dt.float8_e4m3fn_x4
ALU = mybir.AluOpType
ACT = mybir.ActivationFunctionType

P = 128
PACK = 4
PASSES = K // (P * PACK)
QUADRANT = 32
SCALE_ROWS = 4
LIST_ROWS = 16
HALF = S // 2
PIECE = HALF // 2
STATES = V // 2
TERM_PITCH = 8
YG_GROUPS = ((0, 0, PIECE), (0, PIECE, HALF), (1, 0, HALF))


def tile_picked_ycbf_sum_p_kernel(tc, x_words, x_scales, w1, w2, unom, offs, out):
    nc = tc.nc
    with ExitStack() as ctx:
        sb = ctx.enter_context(tc.tile_pool(name="sb", bufs=1))
        ps = ctx.enter_context(tc.psum_pool(name="ps", bufs=1))

        offsets = sb.tile([P, S // LIST_ROWS], U16, name="offsets")
        table_scales = sb.tile([P, T], U8, name="table_scales", tag="scale_table", align_bytes=64)
        table_words = [sb.tile([P, T], U32, name=f"table_words{g}", align_bytes=64) for g in range(PASSES)]
        w2_raw = sb.tile([P, PASSES, PACK * N], F32, name="w2_raw")
        w1_raw = [sb.tile([P, PACK * N], F32, name=f"w1_raw{g}", tag=f"w1_raw{g}") for g in range(PASSES)]
        u = sb.tile([P, V], F32, name="u")
        one = sb.tile([P, 1], F32, name="one")
        inv_weight = sb.tile([P, 1], F32, name="inv_weight")

        nc.vector.memset(table_scales[:].bitcast(I32), 0)
        nc.vector.memset(one[:], 1.0)

        def load_words(g):
            nc.sync.dma_start(table_words[g][:].bitcast(I32), x_words[g].rearrange("p n t -> p (n t)").bitcast(I32))

        def load_scales(r):
            for g in range(PASSES):
                nc.sync.dma_start(
                    table_scales[SCALE_ROWS * g + r : P : QUADRANT, :].bitcast(I32),
                    x_scales[g, r : P // 8 : SCALE_ROWS, :].bitcast(I32),
                )

        nc.sync.dma_start(w2_raw[:], w2.rearrange("(g p j) m -> p g (j m)", g=PASSES, j=PACK))
        nc.sync.dma_start(offsets[:], offs)
        load_scales(0)
        load_words(0)
        for r in range(1, SCALE_ROWS):
            load_scales(r)
        load_words(1)
        nc.scalar.activation(inv_weight[:], one[:], ACT.Abs_reciprocal_sqrt, scale=0.8 * 0.8)
        nc.sync.dma_start(u[:], unom)
        w1_passes = w1.rearrange("(g p j) m -> g p (j m)", g=PASSES, j=PACK)
        for g in range(PASSES):
            nc.sync.dma_start(w1_raw[g][:], w1_passes[g])

        w2_bf = sb.tile([P, PASSES, N, PACK], BF16, name="w2_bf", align_bytes=64)
        for g in range(PASSES):
            nc.scalar.copy(w2_bf[:, g, :, :], w2_raw[:, g, :].rearrange("p (j m) -> p m j", j=PACK))
        w2_codes = sb.tile([P, PASSES * N], U32, name="w2_codes", align_bytes=64)
        w2_scales = sb.tile([P, PASSES * N], U8, name="w2_scales", align_bytes=64)
        nc.vector.quantize_mx(
            out=w2_codes[:].bitcast(FP8X4), scales=w2_scales[:], in_=w2_bf[:].rearrange("p g m j -> p (g m j)")
        )

        picked_scales = sb.tile([P, S], U8, name="picked_scales", align_bytes=64)
        nc.vector.tensor_copy(picked_scales[:], table_scales[:].indirect(offsets[:]))
        picked0 = sb.tile([P, S], U32, name="picked0", align_bytes=64)
        nc.vector.tensor_copy(picked0[:], table_words[0][:].indirect(offsets[:]))
        picked1 = sb.tile([P, S], U32, name="picked1", tag="scale_table", align_bytes=64)
        picked = [picked0, picked1]

        yg = [ps.tile([P, b - a], F32, name=f"yg{i}") for i, (h, a, b) in enumerate(YG_GROUPS)]
        yh = ps.tile([P, S], F32, name="yh")
        square = sb.tile([P, HALF], F32, name="square")
        root = [sb.tile([P, HALF], F32, name=f"root{h}") for h in range(2)]

        def mx_pass(acc, codes, scales, g, cols):
            nc.tensor.matmul_mx(
                out=acc,
                lhsT=codes.bitcast(FP8X4),
                lhsT_scale=scales,
                rhs=picked[g][:, cols].bitcast(FP8X4),
                rhs_scale=picked_scales[SCALE_ROWS * g : P, cols],
                start=(g == 0),
                stop=(g == PASSES - 1),
            )

        for i, (h, a, b) in enumerate(YG_GROUPS):
            mx_pass(yg[i][:], w2_codes[:, 0:N], w2_scales[:, 0:N], 0, slice(h * HALF + a, h * HALF + b))
        for h in range(2):
            nc.vector.tensor_copy(
                picked1[:, h * HALF : (h + 1) * HALF],
                table_words[1][:].indirect(offsets[:, h * HALF // LIST_ROWS : (h + 1) * HALF // LIST_ROWS]),
            )
            for i, (group_half, a, b) in enumerate(YG_GROUPS):
                if group_half == h:
                    cols = slice(h * HALF + a, h * HALF + b)
                    mx_pass(yg[i][:], w2_codes[:, N : 2 * N], w2_scales[:, N : 2 * N], 1, cols)
                    for c in range(a, b, PIECE):
                        nc.scalar.activation(square[:, c : c + PIECE], yg[i][:, c - a : c - a + PIECE], ACT.Square)
            for c in range(0, HALF, PIECE):
                nc.scalar.activation(
                    root[h][:, c : c + PIECE], square[:, c : c + PIECE], ACT.Abs_reciprocal_sqrt, bias=0.3
                )

        w1_bf = [sb.tile([P, N, PACK], BF16, name=f"w1_bf{g}", tag=f"w1_bf{g}", align_bytes=64) for g in range(PASSES)]
        w1_codes = [sb.tile([P, N], U32, name=f"w1_codes{g}", align_bytes=64) for g in range(PASSES)]
        w1_scales = [sb.tile([P, N], U8, name=f"w1_scales{g}", align_bytes=64) for g in range(PASSES)]
        for g in range(PASSES):
            nc.vector.tensor_copy(w1_bf[g][:], w1_raw[g][:].rearrange("p (j m) -> p m j", j=PACK))
        for g in range(PASSES):
            nc.vector.quantize_mx(
                out=w1_codes[g][:].bitcast(FP8X4), scales=w1_scales[g][:], in_=w1_bf[g][:].rearrange("p m j -> p (m j)")
            )
            mx_pass(yh[:], w1_codes[g][:], w1_scales[g][:], g, slice(0, S))

        terms = sb.tile([P, V, TERM_PITCH], F32, name="terms", tag="w1_raw0")
        nc.vector.tensor_copy(terms[:, :, D], u[:])
        push0 = sb.tile([P, HALF], F32, name="push0", tag="w1_raw1")
        after_w1 = sb.tile([P, 3, HALF], F32, name="after_w1", tag="w1_bf1", align_bytes=64)
        push = [push0[:], after_w1[:, 0, :]]
        slope = [after_w1[:, 1, :], after_w1[:, 2, :]]
        gain = [sb.tile([P, HALF], F32, name=f"gain{h}") for h in range(2)]
        bar = [sb.tile([P, HALF], F32, name=f"bar{h}") for h in range(2)]
        slack = [sb.tile([P, HALF], F32, name=f"slack{h}") for h in range(2)]
        result = [sb.tile([P, STATES], F32, name=f"result{h}") for h in range(2)]

        def by_state(ap):
            return ap.rearrange("p (v d) -> p v d", d=D)

        for i, (h, a, b) in enumerate(YG_GROUPS):
            states = slice((h * HALF + a) // D, (h * HALF + b) // D)
            nc.vector.scalar_tensor_tensor(
                by_state(push[h][:, a:b]),
                by_state(yg[i][:]),
                inv_weight[:],
                u[:, states].unsqueeze(2).to_broadcast([P, (b - a) // D, D]),
                ALU.mult,
                ALU.mult,
            )
            nc.vector.tensor_tensor(slope[h][:, a:b], yg[i][:], root[h][:, a:b], ALU.mult)
        for h in range(2):
            nc.vector.scalar_tensor_tensor(gain[h][:], slope[h], -0.8, root[h][:], ALU.mult, ALU.mult)
        for h in range(2):
            nc.scalar.activation(bar[h][:], yh[:, h * HALF : (h + 1) * HALF], ACT.Exp, scale=0.4)
        for h in range(2):
            nc.vector.scalar_tensor_tensor(slack[h][:], push[h], 1.0, bar[h][:], ALU.subtract, ALU.add)
        for h in range(2):
            states = slice(h * STATES, (h + 1) * STATES)
            nc.vector.scalar_tensor_tensor(
                terms[:, states, 0:D], by_state(slack[h][:]), 0.0, by_state(gain[h][:]), ALU.min, ALU.mult
            )
        for h in range(2):
            states = slice(h * STATES, (h + 1) * STATES)
            nc.vector.tensor_reduce(result[h][:], terms[:, states, 0 : D + 1], mybir.AxisListType.X, ALU.add)
            nc.sync.dma_start(out[:, states], result[h][:])
